import numpy as np
import ml_dtypes


def mxq(x, axis, fmt="e4m3"):
    dtype, down = {"e4m3": (ml_dtypes.float8_e4m3fn, 7), "e5m2": (ml_dtypes.float8_e5m2, 14)}[fmt]
    v = np.moveaxis(np.asarray(x, np.float32).astype(ml_dtypes.bfloat16).astype(np.float64), axis, -1)
    blocks = v.reshape(v.shape[:-1] + (-1, 32))
    amax = np.abs(blocks).max(-1, keepdims=True)
    byte = np.maximum(np.where(amax > 0, np.frexp(amax)[1] - 1 + 127, 0) - down, 1)
    scale = np.exp2(byte - 127.0)
    codes = (blocks / scale).astype(np.float32).astype(dtype).astype(np.float64)
    return np.moveaxis((codes * scale).reshape(v.shape), -1, axis)


WIDE = False


def mx_kscale(k):
    if not WIDE:
        return np.ones(k)
    levels = np.array([10, -10, 5, -5, 0])
    if k % 512:
        return np.exp2(np.random.permutation(np.resize(levels, k // 32))).repeat(32)
    a = np.empty((k // 512, 16))
    for p in range(k // 512):
        a[p, :8] = np.random.permutation(np.resize(levels, 8))
        for g in range(8):
            far = levels[np.abs(levels - a[p, g]) >= 10]
            a[p, g + 8] = far[np.random.randint(len(far))]
    return np.exp2(a.ravel()).repeat(32)


def f64(x):
    return np.asarray(x).astype(np.float64)


def striped(idx):
    return np.tile(idx.reshape(-1, 16).T, (8, 1)).astype(np.uint16)


def unstriped(offs):
    return offs[:16].T.reshape(-1).astype(np.int64)


def striped8(idx):
    return np.concatenate([x.reshape(-1, 16).T for x in idx]).astype(np.uint16)


def runs(offs, k):
    lists = np.stack([offs[16 * r : 16 * r + 16].T.reshape(-1) for r in range(8)]).astype(np.int64)
    return lists[np.arange(k) % 512 // 64]


def pack_weight(w):
    k, n = w.shape
    w = f64(np.asarray(w, np.float32).astype(ml_dtypes.bfloat16)).reshape(k // 32, 32, n)
    amax = np.abs(w).max(1)
    byte = np.clip(np.where(amax > 0, np.frexp(amax)[1] - 1 + 127 - 7, 1), 1, 254)
    scaled = (w * np.exp2(127.0 - byte)[:, None, :]).reshape(k, n).astype(np.float32)
    words = np.ascontiguousarray(scaled.reshape(k // 512, 128, 4, n).transpose(0, 1, 3, 2)).astype(ml_dtypes.float8_e4m3fn).view(np.uint8)
    return words, np.ascontiguousarray(byte.astype(np.uint8).reshape(k // 512, 16, n))


def unpack_weight(words, scales):
    g, p, n, _ = words.shape
    vals = np.ascontiguousarray(words).view(ml_dtypes.float8_e4m3fn).astype(np.float64) * np.repeat(np.exp2(scales.astype(np.float64) - 127.0), 8, axis=1)[..., None]
    return vals.transpose(0, 1, 3, 2).reshape(g * 512, n)


def sigmoid(v):
    return 1.0 / (1.0 + np.exp(-np.maximum(v, -700.0)))

def planes(y):
    n, m = y.shape
    v = y.astype(np.float32).astype(ml_dtypes.bfloat16).astype(np.float64).reshape(n // 32, 32, m)
    top = np.abs(v).max(1)
    byte = np.clip(np.where(top > 0, np.frexp(top)[1] - 1 + 127 - 7, 1), 1, 254)
    codes = (v * np.exp2(127.0 - byte)[:, None, :]).reshape(n, m).astype(np.float32).astype(ml_dtypes.float8_e4m3fn).view(np.uint8)
    words = codes.reshape(n // 512, 128, 4, m).transpose(0, 1, 3, 2)
    return np.ascontiguousarray(words), np.ascontiguousarray(byte.astype(np.uint8).reshape(n // 512, 16, m))


K, T, S, V, G, H, C, W = 512, 2048, 1024, 512, 2048, 512, 512, 256


def setup_inputs():
    n = np.random.standard_normal
    s = mx_kscale(K)[:, None]
    packed_xT = pack_weight(n((K, T)) * s)
    packed_dT = pack_weight(n((K, G)) / s)
    perm = np.stack([np.random.permutation(V) for _ in range(8)])
    return {
        "x_words": packed_xT[0],
        "x_scales": packed_xT[1],
        "d_words": packed_dT[0],
        "d_scales": packed_dT[1],
        "gs": (np.random.uniform(0.5, 1.5, (K, 1)) / s).astype(np.float32),
        "offs": striped(np.random.permutation(T)[:S]),
        "k1": striped8(np.random.randint(0, G, (8, H))),
        "n1": striped8(np.stack([np.random.permutation(S) for _ in range(8)])),
        "cand": striped(np.random.permutation(T)[:C]),
        "n2": striped8(perm[:, :W]),
        "n3": striped8(perm[:, W:]),
    }


def reference(x_words, x_scales, d_words, d_scales, gs, offs, k1, n1, cand, n2, n3):
    x_cand = unpack_weight(x_words, x_scales)[:, unstriped(cand)]
    d_k1 = unpack_weight(d_words, d_scales)[np.arange(K)[:, None], runs(k1, K)]
    xq = unpack_weight(x_words, x_scales)[:, unstriped(offs)]
    h = 0.0625 * (d_k1.T @ xq)
    ln = h[np.arange(H)[:, None], runs(n1, H)]
    mx = ln.reshape(H, V, 2).max(axis=2)
    mn = ln.reshape(H, V, 2).min(axis=2)
    z = f64(gs) * (mx * sigmoid(mn))
    s = 0.0625 * ((x_cand.T @ mxq(z, 0, "e4m3")))
    pa = s[np.arange(C)[:, None], runs(n2, C)]
    pb = s[np.arange(C)[:, None], runs(n3, C)]
    rb = np.minimum(pa, pb)
    ra = np.maximum(pa, pb)
    ds = np.zeros((C, V))
    ds[np.arange(C)[:, None], runs(n2, C)] = ra
    out = ds.copy()
    out[np.arange(C)[:, None], runs(n3, C)] = rb
    return (out,) + planes(out)

@@ -1,0 +1,190 @@
+from contextlib import ExitStack
+
+import concourse.mybir as mybir
+
+F32 = mybir.dt.float32
+BF16 = mybir.dt.bfloat16
+I32 = mybir.dt.int32
+U32 = mybir.dt.uint32
+U16 = mybir.dt.uint16
+U8 = mybir.dt.uint8
+FP8X4 = mybir.dt.float8_e4m3fn_x4
+ACT = mybir.ActivationFunctionType
+ALU = mybir.AluOpType
+
+P = 128
+PACK = 4
+T = 2048
+S = 1024
+V = 512
+W = 256
+HALF = 512
+ZC = HALF // 2
+SCALE = 0.0625
+Z_SPLIT = 176
+Y_SPLIT = 336
+
+FLOPS = 2 * 512 * 512 * (1024 + 512)
+
+
+def tile_picked_pqcpgateorder_none_po_kernel(
+    tc, x_words, x_scales, d_words, d_scales, gs, offs, k1, n1, cand, n2, n3, out_0, out_1, out_2
+):
+    nc = tc.nc
+    with ExitStack() as ctx:
+        keep = ctx.enter_context(tc.tile_pool(name="keep", bufs=1))
+        ring = ctx.enter_context(tc.tile_pool(name="ring", bufs=3))
+        psum = ctx.enter_context(tc.psum_pool(name="psum", bufs=2))
+
+        def load_list(name, src):
+            tile = keep.tile(list(src.shape), U16, name=name)
+            nc.sync.dma_start(tile[:], src)
+            return tile
+
+        def words_view(dram):
+            return dram[0].rearrange("p n t -> p (n t)").bitcast(I32)
+
+        def deal(dealt, gathered):
+            nc.vector.tensor_copy(dealt.rearrange("p (t m) -> p t m", t=PACK), gathered[:].rearrange("p (m t) -> p t m", t=PACK))
+
+        def deal_words(dealt, gathered):
+            nc.vector.tensor_copy(
+                dealt.rearrange("p (t a i) -> p a t i", t=PACK, i=4), gathered[:].rearrange("p (a i t) -> p a t i", t=PACK, i=4)
+            )
+
+        d_bytes = keep.tile([P, T], U8, name="d_bytes")
+        x_bytes = keep.tile([P, T], U8, name="x_bytes")
+        nc.gpsimd.memset(d_bytes[:].bitcast(I32), 0)
+        nc.vector.memset(x_bytes[:].bitcast(I32), 0)
+
+        k1_t = load_list("k1_t", k1)
+        nc.sync.dma_start(d_bytes[0:P:8, :].bitcast(I32), d_scales[0].bitcast(I32))
+        offs_t = load_list("offs_t", offs)
+        nc.sync.dma_start(x_bytes[0:P:8, :].bitcast(I32), x_scales[0].bitcast(I32))
+        cand_t = load_list("cand_t", cand)
+        n1_t = load_list("n1_t", n1)
+        d_tab = keep.tile([P, T], I32, name="d_tab")
+        x_tab = keep.tile([P, T], I32, name="x_tab")
+        nc.sync.dma_start(d_tab[:], words_view(d_words))
+        nc.sync.dma_start(x_tab[:], words_view(x_words))
+        n2_t = load_list("n2_t", n2)
+        n3_t = load_list("n3_t", n3)
+        gain = keep.tile([P, PACK], F32, name="gain")
+        nc.gpsimd.dma_start(gain[:], gs.rearrange("(p t) o -> p (t o)", t=PACK))
+
+        warm = keep.tile([P, 1], F32, name="warm")
+        nc.scalar.activation(warm[:], gain[:, 0:1], ACT.Sigmoid)
+
+        def gather(name, table, offsets, n, dtype):
+            got = keep.tile([P, n], dtype, name=name, align_bytes=64)
+            nc.vector.tensor_copy(got[:], table.indirect(offsets))
+            return got
+
+        planes = keep.tile([P, 512 + S + 512], U8, name="planes", align_bytes=64)
+        dk_bytes, xo_bytes, xc_bytes = planes[:, :512], planes[:, 512 : 512 + S], planes[:, 512 + S :]
+        deal(dk_bytes, gather("dk_bytes_raw", d_bytes[:], k1_t[:], 512, U8))
+        nc.vector.tensor_copy(xo_bytes.bitcast(I32), gather("xo_bytes_raw", x_bytes[:], offs_t[:], S, U8)[:].bitcast(I32))
+        deal(xc_bytes, gather("xc_bytes_raw", x_bytes[:], cand_t[:], 512, U8))
+        for j in range(1, 4):
+            nc.scalar.dma_start(planes[j:P:32, :].bitcast(I32), planes[8 * j : P : 32, :].bitcast(I32))
+        dk_words = keep.tile([P, 512], U32, name="dk_words", align_bytes=64)
+        xc_words = keep.tile([P, 512], U32, name="xc_words", align_bytes=64)
+        deal_words(dk_words[:], gather("dk_words_raw", d_tab[:].bitcast(U32), k1_t[:], 512, U32))
+        xo_words = [
+            gather("xo_words%d" % c, x_tab[:].bitcast(U32), offs_t[:, 32 * c : 32 * (c + 1)], HALF, U32) for c in range(2)
+        ]
+        deal_words(xc_words[:], gather("xc_words_raw", x_tab[:].bitcast(U32), cand_t[:], 512, U32))
+
+        h = [keep.tile([P, S], F32, name="h%d" % t) for t in range(PACK)]
+        for t in range(PACK):
+            for c in range(2):
+                h_bank = psum.tile([P, HALF], F32, name="h_bank", bufs=6)
+                nc.tensor.matmul_mx(
+                    h_bank[:],
+                    lhsT=dk_words[:, P * t : P * (t + 1)].bitcast(FP8X4),
+                    lhsT_scale=dk_bytes[:, P * t : P * (t + 1)],
+                    rhs=xo_words[c][:].bitcast(FP8X4),
+                    rhs_scale=xo_bytes[:, HALF * c : HALF * (c + 1)],
+                    start=True,
+                    stop=True,
+                )
+                nc.scalar.activation(h[t][:, HALF * c : HALF * (c + 1)], h_bank[:], ACT.Copy, scale=SCALE)
+
+        s = [keep.tile([P, V], F32, name="s%d" % t) for t in range(PACK)]
+        for c in range(2):
+            z_rows = keep.tile([P, PACK, ZC], BF16, name="z_rows%d" % c)
+            for t in range(PACK):
+                ln = ring.tile([P, HALF], F32, name="ln")
+                nc.vector.tensor_copy(ln[:], h[t][:].indirect(n1_t[:, 32 * c : 32 * (c + 1)]))
+                mn = ring.tile([P, ZC], F32, name="mn")
+                mx = ring.tile([P, ZC], F32, name="mx")
+                sg = ring.tile([P, ZC], F32, name="sg")
+                nc.vector.tensor_tensor(mn[:], ln[:, 0::2], ln[:, 1::2], ALU.min)
+                nc.vector.tensor_tensor(mx[:], ln[:, 0::2], ln[:, 1::2], ALU.max)
+                nc.scalar.activation(sg[:], mn[:], ACT.Sigmoid)
+                nc.vector.scalar_tensor_tensor(z_rows[:, t, :], mx[:], gain[:, t : t + 1], sg[:], ALU.mult, ALU.mult)
+            z_packed = keep.tile([P, ZC, PACK], BF16, name="z_packed%d" % c, align_bytes=64)
+            split = Z_SPLIT * c
+            dst = z_packed[:].rearrange("p (a i) t -> p a t i", i=4)
+            src = z_rows[:].rearrange("p t (a i) -> p a t i", i=4)
+            if split:
+                nc.vector.tensor_copy(dst[:, : split // 4], src[:, : split // 4])
+            nc.scalar.copy(dst[:, split // 4 :], src[:, split // 4 :])
+            z_words = keep.tile([P, ZC], U32, name="z_words%d" % c, align_bytes=64)
+            z_bytes = keep.tile([P, ZC], U8, name="z_bytes%d" % c, align_bytes=64)
+            nc.vector.quantize_mx(z_words[:].bitcast(FP8X4), z_bytes[:], z_packed[:].rearrange("p v t -> p (v t)"))
+            for t in range(PACK):
+                s_bank = psum.tile([P, ZC], F32, name="s_bank")
+                nc.tensor.matmul_mx(
+                    s_bank[:],
+                    lhsT=xc_words[:, P * t : P * (t + 1)].bitcast(FP8X4),
+                    lhsT_scale=xc_bytes[:, P * t : P * (t + 1)],
+                    rhs=z_words[:].bitcast(FP8X4),
+                    rhs_scale=z_bytes[:],
+                    start=True,
+                    stop=True,
+                )
+                nc.scalar.activation(s[t][:, ZC * c : ZC * (c + 1)], s_bank[:], ACT.Copy, scale=SCALE)
+
+        y = [keep.tile([P, V], F32, name="y%d" % t) for t in range(PACK)]
+        pa = [keep.tile([P, W], F32, name="pa%d" % t) for t in range(PACK)]
+        pb = [keep.tile([P, W], F32, name="pb%d" % t) for t in range(PACK)]
+        ra = [keep.tile([P, W], F32, name="ra%d" % t) for t in range(PACK)]
+        rb = [keep.tile([P, W], F32, name="rb%d" % t) for t in range(PACK)]
+        y_packed = keep.tile([P, V, PACK], BF16, name="y_packed", align_bytes=64)
+        out_rows = out_0.rearrange("(p t) v -> t p v", t=PACK)
+
+        def fetch(t):
+            nc.vector.tensor_copy(pa[t][:], s[t][:].indirect(n2_t[:]))
+            nc.vector.tensor_copy(pb[t][:], s[t][:].indirect(n3_t[:]))
+
+        def order(t):
+            nc.vector.tensor_tensor(ra[t][:], pa[t][:], pb[t][:], ALU.max)
+            nc.vector.tensor_tensor(rb[t][:], pa[t][:], pb[t][:], ALU.min)
+
+        def put_larger(t):
+            nc.vector.tensor_copy(y[t][:].indirect(n2_t[:]), ra[t][:])
+
+        def put_smaller(t):
+            nc.vector.tensor_copy(y[t][:].indirect(n3_t[:]), rb[t][:])
+            nc.sync.dma_start(out_rows[t], y[t][:])
+            if t < 2:
+                nc.scalar.copy(y_packed[:, :, t], y[t][:])
+            elif t == 2:
+                nc.scalar.copy(y_packed[:, :, 2:4], y[t][:].unsqueeze(2).to_broadcast([P, V, 2]))
+            else:
+                nc.vector.tensor_copy(y_packed[:, :Y_SPLIT, t], y[t][:, :Y_SPLIT])
+                nc.scalar.copy(y_packed[:, Y_SPLIT:, t], y[t][:, Y_SPLIT:])
+
+        for t0 in (0, 2):
+            for step in (fetch, order, put_larger, put_smaller):
+                step(t0)
+                step(t0 + 1)
+
+        y_words = keep.tile([P, V], I32, name="y_words", align_bytes=64)
+        y_bytes = keep.tile([P, V], U8, name="y_bytes", align_bytes=64)
+        nc.vector.quantize_mx(y_words[:].bitcast(FP8X4), y_bytes[:], y_packed[:].rearrange("p v t -> p (v t)"))
+        nc.sync.dma_start(words_view(out_1), y_words[:])
+        for q in range(4):
+            queue = nc.scalar if q < 2 else nc.sync
+            queue.dma_start(out_2[0][4 * q : 4 * q + 4, :].bitcast(I32), y_bytes[32 * q : 32 * q + 4, :].bitcast(I32))

@@ -22,7 +22,7 @@ HALF = 512
 ZC = HALF // 2
 SCALE = 0.0625
 Z_SPLIT = 176
-Y_SPLIT = 336
+Y_SPLIT = 256
 
 FLOPS = 2 * 512 * 512 * (1024 + 512)
 
@@ -70,7 +70,7 @@ def tile_picked_pqcpgateorder_none_po_kernel(
         n2_t = load_list("n2_t", n2)
         n3_t = load_list("n3_t", n3)
         gain = keep.tile([P, PACK], F32, name="gain")
-        nc.gpsimd.dma_start(gain[:], gs.rearrange("(p t) o -> p (t o)", t=PACK))
+        nc.scalar.dma_start(gain[:], gs.rearrange("(p t) o -> p (t o)", t=PACK))
 
         warm = keep.tile([P, 1], F32, name="warm")
         nc.scalar.activation(warm[:], gain[:, 0:1], ACT.Sigmoid)
@@ -148,25 +148,27 @@ def tile_picked_pqcpgateorder_none_po_kernel(
 
         y = [keep.tile([P, V], F32, name="y%d" % t) for t in range(PACK)]
         pa = [keep.tile([P, W], F32, name="pa%d" % t) for t in range(PACK)]
-        pb = [keep.tile([P, W], F32, name="pb%d" % t) for t in range(PACK)]
-        ra = [keep.tile([P, W], F32, name="ra%d" % t) for t in range(PACK)]
-        rb = [keep.tile([P, W], F32, name="rb%d" % t) for t in range(PACK)]
+        gap = [keep.tile([P, W], F32, name="gap%d" % t) for t in range(PACK)]
+        up = [keep.tile([P, W], F32, name="up%d" % t) for t in range(PACK)]
+        down = [keep.tile([P, W], F32, name="down%d" % t) for t in range(PACK)]
         y_packed = keep.tile([P, V, PACK], BF16, name="y_packed", align_bytes=64)
         out_rows = out_0.rearrange("(p t) v -> t p v", t=PACK)
 
         def fetch(t):
             nc.vector.tensor_copy(pa[t][:], s[t][:].indirect(n2_t[:]))
-            nc.vector.tensor_copy(pb[t][:], s[t][:].indirect(n3_t[:]))
 
-        def order(t):
-            nc.vector.tensor_tensor(ra[t][:], pa[t][:], pb[t][:], ALU.max)
-            nc.vector.tensor_tensor(rb[t][:], pa[t][:], pb[t][:], ALU.min)
+        def compare(t):
+            nc.vector.tensor_tensor(gap[t][:], s[t][:].indirect(n3_t[:]), pa[t][:], ALU.subtract)
+            fall = ring.tile([P, W], F32, name="fall")
+            nc.scalar.activation(up[t][:], gap[t][:], ACT.Relu)
+            nc.scalar.activation(fall[:], gap[t][:], ACT.Relu, scale=-1.0)
+            nc.scalar.activation(down[t][:], fall[:], ACT.Copy, scale=-1.0)
 
         def put_larger(t):
-            nc.vector.tensor_copy(y[t][:].indirect(n2_t[:]), ra[t][:])
+            nc.vector.tensor_tensor(y[t][:].indirect(n2_t[:]), pa[t][:], up[t][:], ALU.add)
 
         def put_smaller(t):
-            nc.vector.tensor_copy(y[t][:].indirect(n3_t[:]), rb[t][:])
+            nc.vector.tensor_tensor(y[t][:].indirect(n3_t[:]), pa[t][:], down[t][:], ALU.add)
             nc.sync.dma_start(out_rows[t], y[t][:])
             if t < 2:
                 nc.scalar.copy(y_packed[:, :, t], y[t][:])
@@ -177,14 +179,19 @@ def tile_picked_pqcpgateorder_none_po_kernel(
                 nc.scalar.copy(y_packed[:, Y_SPLIT:, t], y[t][:, Y_SPLIT:])
 
         for t0 in (0, 2):
-            for step in (fetch, order, put_larger, put_smaller):
+            for step in (fetch, compare):
+                step(t0)
+                step(t0 + 1)
+        for t0 in (0, 2):
+            for step in (put_larger, put_smaller):
                 step(t0)
                 step(t0 + 1)
 
         y_words = keep.tile([P, V], I32, name="y_words", align_bytes=64)
         y_bytes = keep.tile([P, V], U8, name="y_bytes", align_bytes=64)
-        nc.vector.quantize_mx(y_words[:].bitcast(FP8X4), y_bytes[:], y_packed[:].rearrange("p v t -> p (v t)"))
-        nc.sync.dma_start(words_view(out_1), y_words[:])
+        for cols in (slice(0, Y_SPLIT), slice(Y_SPLIT, V)):
+            nc.vector.quantize_mx(y_words[:, cols].bitcast(FP8X4), y_bytes[:, cols], y_packed[:, cols, :].rearrange("p v t -> p (v t)"))
+            nc.sync.dma_start(words_view(out_1)[:, cols], y_words[:, cols])
         for q in range(4):
             queue = nc.scalar if q < 2 else nc.sync
             queue.dma_start(out_2[0][4 * q : 4 * q + 4, :].bitcast(I32), y_bytes[32 * q : 32 * q + 4, :].bitcast(I32))

@@ -23,6 +23,7 @@ ZC = HALF // 2
 SCALE = 0.0625
 Z_SPLIT = 176
 Y_SPLIT = 256
+Y_SHARE = 384
 
 FLOPS = 2 * 512 * 512 * (1024 + 512)
 
@@ -110,6 +111,9 @@ def tile_picked_pqcpgateorder_none_po_kernel(
                 )
                 nc.scalar.activation(h[t][:, HALF * c : HALF * (c + 1)], h_bank[:], ACT.Copy, scale=SCALE)
 
+        sixteenth = [keep.tile([P, 1], F32, name="sixteenth%d" % t, tag="gap%d" % t) for t in range(PACK - 1)]
+        for tile in sixteenth:
+            nc.gpsimd.memset(tile[:], SCALE)
         s = [keep.tile([P, V], F32, name="s%d" % t) for t in range(PACK)]
         for c in range(2):
             z_rows = keep.tile([P, PACK, ZC], BF16, name="z_rows%d" % c)
@@ -144,11 +148,11 @@ def tile_picked_pqcpgateorder_none_po_kernel(
                     start=True,
                     stop=True,
                 )
-                nc.scalar.activation(s[t][:, ZC * c : ZC * (c + 1)], s_bank[:], ACT.Copy, scale=SCALE)
+                nc.scalar.activation(s[t][:, ZC * c : ZC * (c + 1)], s_bank[:], ACT.Copy, scale=sixteenth[t - 1][:] if c and t else SCALE)
 
         y = [keep.tile([P, V], F32, name="y%d" % t) for t in range(PACK)]
         pa = [keep.tile([P, W], F32, name="pa%d" % t) for t in range(PACK)]
-        gap = [keep.tile([P, W], F32, name="gap%d" % t) for t in range(PACK)]
+        gap = [keep.tile([P, W], F32, name="gap%d" % t, tag="gap%d" % t) for t in range(PACK)]
         up = [keep.tile([P, W], F32, name="up%d" % t) for t in range(PACK)]
         down = [keep.tile([P, W], F32, name="down%d" % t) for t in range(PACK)]
         y_packed = keep.tile([P, V, PACK], BF16, name="y_packed", align_bytes=64)
@@ -159,8 +163,12 @@ def tile_picked_pqcpgateorder_none_po_kernel(
 
         def compare(t):
             nc.vector.tensor_tensor(gap[t][:], s[t][:].indirect(n3_t[:]), pa[t][:], ALU.subtract)
-            fall = ring.tile([P, W], F32, name="fall")
+
+        def rise(t):
             nc.scalar.activation(up[t][:], gap[t][:], ACT.Relu)
+
+        def drop(t):
+            fall = ring.tile([P, W], F32, name="fall")
             nc.scalar.activation(fall[:], gap[t][:], ACT.Relu, scale=-1.0)
             nc.scalar.activation(down[t][:], fall[:], ACT.Copy, scale=-1.0)
 
@@ -176,10 +184,16 @@ def tile_picked_pqcpgateorder_none_po_kernel(
                 nc.scalar.copy(y_packed[:, :, 2:4], y[t][:].unsqueeze(2).to_broadcast([P, V, 2]))
             else:
                 nc.vector.tensor_copy(y_packed[:, :Y_SPLIT, t], y[t][:, :Y_SPLIT])
-                nc.scalar.copy(y_packed[:, Y_SPLIT:, t], y[t][:, Y_SPLIT:])
+                nc.vector.tensor_copy(y_packed[:, Y_SPLIT:Y_SHARE, t], y[t][:, Y_SPLIT:Y_SHARE])
+                nc.scalar.copy(y_packed[:, Y_SHARE:, t], y[t][:, Y_SHARE:])
 
+        for t in range(PACK + 1):
+            if t < PACK:
+                fetch(t)
+            if t > 0:
+                compare(t - 1)
         for t0 in (0, 2):
-            for step in (fetch, compare):
+            for step in (rise, drop):
                 step(t0)
                 step(t0 + 1)
         for t0 in (0, 2):

from contextlib import ExitStack

import concourse.mybir as mybir

F32 = mybir.dt.float32
BF16 = mybir.dt.bfloat16
I32 = mybir.dt.int32
U32 = mybir.dt.uint32
U16 = mybir.dt.uint16
U8 = mybir.dt.uint8
FP8X4 = mybir.dt.float8_e4m3fn_x4
ACT = mybir.ActivationFunctionType
ALU = mybir.AluOpType

P = 128
PACK = 4
T = 2048
S = 1024
V = 512
W = 256
HALF = 512
ZC = HALF // 2
SCALE = 0.0625
Z_SPLIT = 176
Y_SPLIT = 256
Y_SHARE = 384

FLOPS = 2 * 512 * 512 * (1024 + 512)


def tile_picked_pqcpgateorder_none_po_kernel(
    tc, x_words, x_scales, d_words, d_scales, gs, offs, k1, n1, cand, n2, n3, out_0, out_1, out_2
):
    nc = tc.nc
    with ExitStack() as ctx:
        keep = ctx.enter_context(tc.tile_pool(name="keep", bufs=1))
        ring = ctx.enter_context(tc.tile_pool(name="ring", bufs=3))
        psum = ctx.enter_context(tc.psum_pool(name="psum", bufs=2))

        def load_list(name, src):
            tile = keep.tile(list(src.shape), U16, name=name)
            nc.sync.dma_start(tile[:], src)
            return tile

        def words_view(dram):
            return dram[0].rearrange("p n t -> p (n t)").bitcast(I32)

        def deal(dealt, gathered):
            nc.vector.tensor_copy(dealt.rearrange("p (t m) -> p t m", t=PACK), gathered[:].rearrange("p (m t) -> p t m", t=PACK))

        def deal_words(dealt, gathered):
            nc.vector.tensor_copy(
                dealt.rearrange("p (t a i) -> p a t i", t=PACK, i=4), gathered[:].rearrange("p (a i t) -> p a t i", t=PACK, i=4)
            )

        d_bytes = keep.tile([P, T], U8, name="d_bytes")
        x_bytes = keep.tile([P, T], U8, name="x_bytes")
        nc.gpsimd.memset(d_bytes[:].bitcast(I32), 0)
        nc.vector.memset(x_bytes[:].bitcast(I32), 0)

        k1_t = load_list("k1_t", k1)
        nc.sync.dma_start(d_bytes[0:P:8, :].bitcast(I32), d_scales[0].bitcast(I32))
        offs_t = load_list("offs_t", offs)
        nc.sync.dma_start(x_bytes[0:P:8, :].bitcast(I32), x_scales[0].bitcast(I32))
        cand_t = load_list("cand_t", cand)
        n1_t = load_list("n1_t", n1)
        d_tab = keep.tile([P, T], I32, name="d_tab")
        x_tab = keep.tile([P, T], I32, name="x_tab")
        nc.sync.dma_start(d_tab[:], words_view(d_words))
        nc.sync.dma_start(x_tab[:], words_view(x_words))
        n2_t = load_list("n2_t", n2)
        n3_t = load_list("n3_t", n3)
        gain = keep.tile([P, PACK], F32, name="gain")
        nc.scalar.dma_start(gain[:], gs.rearrange("(p t) o -> p (t o)", t=PACK))

        warm = keep.tile([P, 1], F32, name="warm")
        nc.scalar.activation(warm[:], gain[:, 0:1], ACT.Sigmoid)

        def gather(name, table, offsets, n, dtype):
            got = keep.tile([P, n], dtype, name=name, align_bytes=64)
            nc.vector.tensor_copy(got[:], table.indirect(offsets))
            return got

        planes = keep.tile([P, 512 + S + 512], U8, name="planes", align_bytes=64)
        dk_bytes, xo_bytes, xc_bytes = planes[:, :512], planes[:, 512 : 512 + S], planes[:, 512 + S :]
        deal(dk_bytes, gather("dk_bytes_raw", d_bytes[:], k1_t[:], 512, U8))
        nc.vector.tensor_copy(xo_bytes.bitcast(I32), gather("xo_bytes_raw", x_bytes[:], offs_t[:], S, U8)[:].bitcast(I32))
        deal(xc_bytes, gather("xc_bytes_raw", x_bytes[:], cand_t[:], 512, U8))
        for j in range(1, 4):
            nc.scalar.dma_start(planes[j:P:32, :].bitcast(I32), planes[8 * j : P : 32, :].bitcast(I32))
        dk_words = keep.tile([P, 512], U32, name="dk_words", align_bytes=64)
        xc_words = keep.tile([P, 512], U32, name="xc_words", align_bytes=64)
        deal_words(dk_words[:], gather("dk_words_raw", d_tab[:].bitcast(U32), k1_t[:], 512, U32))
        xo_words = [
            gather("xo_words%d" % c, x_tab[:].bitcast(U32), offs_t[:, 32 * c : 32 * (c + 1)], HALF, U32) for c in range(2)
        ]
        deal_words(xc_words[:], gather("xc_words_raw", x_tab[:].bitcast(U32), cand_t[:], 512, U32))

        h = [keep.tile([P, S], F32, name="h%d" % t) for t in range(PACK)]
        for t in range(PACK):
            for c in range(2):
                h_bank = psum.tile([P, HALF], F32, name="h_bank", bufs=6)
                nc.tensor.matmul_mx(
                    h_bank[:],
                    lhsT=dk_words[:, P * t : P * (t + 1)].bitcast(FP8X4),
                    lhsT_scale=dk_bytes[:, P * t : P * (t + 1)],
                    rhs=xo_words[c][:].bitcast(FP8X4),
                    rhs_scale=xo_bytes[:, HALF * c : HALF * (c + 1)],
                    start=True,
                    stop=True,
                )
                nc.scalar.activation(h[t][:, HALF * c : HALF * (c + 1)], h_bank[:], ACT.Copy, scale=SCALE)

        sixteenth = [keep.tile([P, 1], F32, name="sixteenth%d" % t, tag="gap%d" % t) for t in range(PACK - 1)]
        for tile in sixteenth:
            nc.gpsimd.memset(tile[:], SCALE)
        s = [keep.tile([P, V], F32, name="s%d" % t) for t in range(PACK)]
        for c in range(2):
            z_rows = keep.tile([P, PACK, ZC], BF16, name="z_rows%d" % c)
            for t in range(PACK):
                ln = ring.tile([P, HALF], F32, name="ln")
                nc.vector.tensor_copy(ln[:], h[t][:].indirect(n1_t[:, 32 * c : 32 * (c + 1)]))
                mn = ring.tile([P, ZC], F32, name="mn")
                mx = ring.tile([P, ZC], F32, name="mx")
                sg = ring.tile([P, ZC], F32, name="sg")
                nc.vector.tensor_tensor(mn[:], ln[:, 0::2], ln[:, 1::2], ALU.min)
                nc.vector.tensor_tensor(mx[:], ln[:, 0::2], ln[:, 1::2], ALU.max)
                nc.scalar.activation(sg[:], mn[:], ACT.Sigmoid)
                nc.vector.scalar_tensor_tensor(z_rows[:, t, :], mx[:], gain[:, t : t + 1], sg[:], ALU.mult, ALU.mult)
            z_packed = keep.tile([P, ZC, PACK], BF16, name="z_packed%d" % c, align_bytes=64)
            split = Z_SPLIT * c
            dst = z_packed[:].rearrange("p (a i) t -> p a t i", i=4)
            src = z_rows[:].rearrange("p t (a i) -> p a t i", i=4)
            if split:
                nc.vector.tensor_copy(dst[:, : split // 4], src[:, : split // 4])
            nc.scalar.copy(dst[:, split // 4 :], src[:, split // 4 :])
            z_words = keep.tile([P, ZC], U32, name="z_words%d" % c, align_bytes=64)
            z_bytes = keep.tile([P, ZC], U8, name="z_bytes%d" % c, align_bytes=64)
            nc.vector.quantize_mx(z_words[:].bitcast(FP8X4), z_bytes[:], z_packed[:].rearrange("p v t -> p (v t)"))
            for t in range(PACK):
                s_bank = psum.tile([P, ZC], F32, name="s_bank")
                nc.tensor.matmul_mx(
                    s_bank[:],
                    lhsT=xc_words[:, P * t : P * (t + 1)].bitcast(FP8X4),
                    lhsT_scale=xc_bytes[:, P * t : P * (t + 1)],
                    rhs=z_words[:].bitcast(FP8X4),
                    rhs_scale=z_bytes[:],
                    start=True,
                    stop=True,
                )
                nc.scalar.activation(s[t][:, ZC * c : ZC * (c + 1)], s_bank[:], ACT.Copy, scale=sixteenth[t - 1][:] if c and t else SCALE)

        y = [keep.tile([P, V], F32, name="y%d" % t) for t in range(PACK)]
        pa = [keep.tile([P, W], F32, name="pa%d" % t) for t in range(PACK)]
        gap = [keep.tile([P, W], F32, name="gap%d" % t, tag="gap%d" % t) for t in range(PACK)]
        up = [keep.tile([P, W], F32, name="up%d" % t) for t in range(PACK)]
        down = [keep.tile([P, W], F32, name="down%d" % t) for t in range(PACK)]
        y_packed = keep.tile([P, V, PACK], BF16, name="y_packed", align_bytes=64)
        out_rows = out_0.rearrange("(p t) v -> t p v", t=PACK)

        def fetch(t):
            nc.vector.tensor_copy(pa[t][:], s[t][:].indirect(n2_t[:]))

        def compare(t):
            nc.vector.tensor_tensor(gap[t][:], s[t][:].indirect(n3_t[:]), pa[t][:], ALU.subtract)

        def rise(t):
            nc.scalar.activation(up[t][:], gap[t][:], ACT.Relu)

        def drop(t):
            fall = ring.tile([P, W], F32, name="fall")
            nc.scalar.activation(fall[:], gap[t][:], ACT.Relu, scale=-1.0)
            nc.scalar.activation(down[t][:], fall[:], ACT.Copy, scale=-1.0)

        def put_larger(t):
            nc.vector.tensor_tensor(y[t][:].indirect(n2_t[:]), pa[t][:], up[t][:], ALU.add)

        def put_smaller(t):
            nc.vector.tensor_tensor(y[t][:].indirect(n3_t[:]), pa[t][:], down[t][:], ALU.add)
            nc.sync.dma_start(out_rows[t], y[t][:])
            if t < 2:
                nc.scalar.copy(y_packed[:, :, t], y[t][:])
            elif t == 2:
                nc.scalar.copy(y_packed[:, :, 2:4], y[t][:].unsqueeze(2).to_broadcast([P, V, 2]))
            else:
                nc.vector.tensor_copy(y_packed[:, :Y_SPLIT, t], y[t][:, :Y_SPLIT])
                nc.vector.tensor_copy(y_packed[:, Y_SPLIT:Y_SHARE, t], y[t][:, Y_SPLIT:Y_SHARE])
                nc.scalar.copy(y_packed[:, Y_SHARE:, t], y[t][:, Y_SHARE:])

        for t in range(PACK + 1):
            if t < PACK:
                fetch(t)
            if t > 0:
                compare(t - 1)
        for t0 in (0, 2):
            for step in (rise, drop):
                step(t0)
                step(t0 + 1)
        for t0 in (0, 2):
            for step in (put_larger, put_smaller):
                step(t0)
                step(t0 + 1)

        y_words = keep.tile([P, V], I32, name="y_words", align_bytes=64)
        y_bytes = keep.tile([P, V], U8, name="y_bytes", align_bytes=64)
        for cols in (slice(0, Y_SPLIT), slice(Y_SPLIT, V)):
            nc.vector.quantize_mx(y_words[:, cols].bitcast(FP8X4), y_bytes[:, cols], y_packed[:, cols, :].rearrange("p v t -> p (v t)"))
            nc.sync.dma_start(words_view(out_1)[:, cols], y_words[:, cols])
        for q in range(4):
            queue = nc.scalar if q < 2 else nc.sync
            queue.dma_start(out_2[0][4 * q : 4 * q + 4, :].bitcast(I32), y_bytes[32 * q : 32 * q + 4, :].bitcast(I32))
